import numpy as np
import ml_dtypes


def mxq(x, axis, fmt="e4m3"):
    dtype, down = {"e4m3": (ml_dtypes.float8_e4m3fn, 7), "e5m2": (ml_dtypes.float8_e5m2, 14)}[fmt]
    v = np.moveaxis(np.asarray(x, np.float32).astype(ml_dtypes.bfloat16).astype(np.float64), axis, -1)
    blocks = v.reshape(v.shape[:-1] + (-1, 32))
    amax = np.abs(blocks).max(-1, keepdims=True)
    byte = np.maximum(np.where(amax > 0, np.frexp(amax)[1] - 1 + 127, 0) - down, 1)
    scale = np.exp2(byte - 127.0)
    codes = (blocks / scale).astype(np.float32).astype(dtype).astype(np.float64)
    return np.moveaxis((codes * scale).reshape(v.shape), -1, axis)


WIDE = False


def mx_kscale(k):
    if not WIDE:
        return np.ones(k)
    levels = np.array([10, -10, 5, -5, 0])
    if k % 512:
        return np.exp2(np.random.permutation(np.resize(levels, k // 32))).repeat(32)
    a = np.empty((k // 512, 16))
    for p in range(k // 512):
        a[p, :8] = np.random.permutation(np.resize(levels, 8))
        for g in range(8):
            far = levels[np.abs(levels - a[p, g]) >= 10]
            a[p, g + 8] = far[np.random.randint(len(far))]
    return np.exp2(a.ravel()).repeat(32)


def f64(x):
    return np.asarray(x).astype(np.float64)


def striped(idx):
    return np.tile(idx.reshape(-1, 16).T, (8, 1)).astype(np.uint16)


def unstriped(offs):
    return offs[:16].T.reshape(-1).astype(np.int64)


def pack_weight(w):
    k, n = w.shape
    w = f64(np.asarray(w, np.float32).astype(ml_dtypes.bfloat16)).reshape(k // 32, 32, n)
    amax = np.abs(w).max(1)
    byte = np.clip(np.where(amax > 0, np.frexp(amax)[1] - 1 + 127 - 7, 1), 1, 254)
    scaled = (w * np.exp2(127.0 - byte)[:, None, :]).reshape(k, n).astype(np.float32)
    words = np.ascontiguousarray(scaled.reshape(k // 512, 128, 4, n).transpose(0, 1, 3, 2)).astype(ml_dtypes.float8_e4m3fn).view(np.uint8)
    return words, np.ascontiguousarray(byte.astype(np.uint8).reshape(k // 512, 16, n))


def unpack_weight(words, scales):
    g, p, n, _ = words.shape
    vals = np.ascontiguousarray(words).view(ml_dtypes.float8_e4m3fn).astype(np.float64) * np.repeat(np.exp2(scales.astype(np.float64) - 127.0), 8, axis=1)[..., None]
    return vals.transpose(0, 1, 3, 2).reshape(g * 512, n)


def relu(v):
    return np.maximum(v, 0.0)


K, T, S, D, H, Z, W = 512, 2048, 512, 2, 512, 512, 2048
P = 2 ** 7


def setup_inputs():
    n = np.random.standard_normal
    s = mx_kscale(K)[:, None]
    packed_xT = pack_weight(n((K, T)) * s)
    packed_eT = pack_weight(n((K, W)) * s)
    return {
        "x_words": packed_xT[0],
        "x_scales": packed_xT[1],
        "w1": (n((K, H)) / np.sqrt(K) / s).astype(np.float32),
        "w2": (n((K, H)) / np.sqrt(K) / s).astype(np.float32),
        "e_words": packed_eT[0],
        "e_scales": packed_eT[1],
        "unit": (np.random.uniform(0.6, 1.4, (K, 1)) / np.sqrt(K) / s).astype(np.float32),
        "price": (np.tile(np.random.uniform(0.2, 1.4, W), (P, 1))).astype(np.float32),
        "offs": striped(np.random.permutation(T)[:S]),
        "sub_": striped(np.random.permutation(S)),
        "off": striped(np.random.permutation(W)[:Z]),
        "cmp": striped(np.random.permutation(Z)),
    }


def reference(x_words, x_scales, w1, w2, e_words, e_scales, unit, price, offs, sub_, off, cmp):
    xq = unpack_weight(x_words, x_scales)[:, unstriped(offs)]
    y = mxq(f64(w1), 0, "e4m3").T @ xq
    yg = mxq(f64(w2), 0, "e4m3").T @ xq
    gs = yg[:, unstriped(sub_)]
    aug = y + 0.6 * gs
    bask = aug.reshape(len(aug), -1, D).sum(axis=2)
    bq = np.tanh(bask) * (np.abs(bask) + 0.4)
    hid = f64(unit) * bq
    e_off = unpack_weight(e_words, e_scales)[:, unstriped(off)]
    sc = mxq(hid, 0, "e4m3").T @ e_off
    syn = sc + 0.5 * sc[:, unstriped(cmp)]
    surp = syn - (f64(price)[:1][:, unstriped(off)])
    return relu(surp) - (0.2 * sc)

@@ -1,0 +1,220 @@
+from contextlib import ExitStack
+
+import concourse.mybir as mybir
+from concourse.masks import make_identity
+
+F32 = mybir.dt.float32
+BF16 = mybir.dt.bfloat16
+I32 = mybir.dt.int32
+U32 = mybir.dt.uint32
+U16 = mybir.dt.uint16
+U8 = mybir.dt.uint8
+FP8X4 = mybir.dt.float8_e4m3fn_x4
+ALU = mybir.AluOpType
+ACT = mybir.ActivationFunctionType
+
+P = 128
+PACK = 4
+K = 512
+TABLE = 2048
+S = 512
+V = 256
+E = 512
+HALF = 128
+FLOPS = 2 * K * 512 * S * 2 + 2 * 512 * V * E
+M_SCALAR = 40
+
+
+def tile_picked_ybundle_surp_p_kernel(
+    tc, x_words, x_scales, w1, w2, e_words, e_scales, unit, price, offs, sub_, off, cmp, out
+):
+    nc = tc.nc
+    with ExitStack() as ctx:
+        lists = ctx.enter_context(tc.tile_pool(name="lists", bufs=1))
+        sb = ctx.enter_context(tc.tile_pool(name="sb", bufs=1))
+        early = ctx.enter_context(tc.tile_pool(name="early", bufs=1))
+        ps = ctx.enter_context(tc.psum_pool(name="ps", bufs=1))
+
+        def load_list(src, name):
+            t = lists.tile([P, 32], U16, name=name)
+            nc.sync.dma_start(t[:], src)
+            return t
+
+        def load_words(src, name, tag):
+            t = sb.tile([P, TABLE], I32, name=name, tag=tag, align_bytes=64)
+            nc.sync.dma_start(t[:], src[0].rearrange("p n t -> p (n t)").bitcast(I32))
+            return t
+
+        def load_scales(t, queues, src):
+            for q in range(4):
+                queues[q].dma_start(t[32 * q : 32 * q + 4, :].bitcast(I32), src[0, 4 * q : 4 * q + 4, :].bitcast(I32))
+
+        def load_weight(src, c0, c1, name, tag):
+            t = sb.tile([P, PACK, c1 - c0], F32, name=name, tag=tag, align_bytes=64)
+            nc.sync.dma_start(t[:], src[:, c0:c1].rearrange("(p j) c -> p j c", j=PACK))
+            return t
+
+        def group_weight(raw, grouped, m0, m1, on_scalar):
+            dst = grouped[:].rearrange("p (t m j) -> p m j t", t=PACK, j=PACK)[:, m0:m1]
+            src = raw[:].rearrange("p j (m t) -> p m j t", t=PACK)
+            if on_scalar:
+                nc.scalar.copy(dst, src)
+            else:
+                nc.vector.tensor_copy(dst, src)
+
+        offs_t = load_list(offs, "offs_t")
+        off_t = load_list(off, "off_t")
+        sub_t = load_list(sub_, "sub_t")
+        cmp_t = load_list(cmp, "cmp_t")
+        xs = sb.tile([P, TABLE], U8, name="xs", tag="xs_w1", align_bytes=64)
+        nc.vector.memset(xs[:].bitcast(I32), 0)
+        load_scales(xs, [nc.scalar] * 4, x_scales)
+        es = early.tile([P, TABLE], U8, name="es", align_bytes=64, offset=512)
+        nc.gpsimd.memset(es[:].bitcast(I32), 0)
+        load_scales(es, [nc.scalar, nc.gpsimd, nc.gpsimd, nc.gpsimd], e_scales)
+        w2_a = load_weight(w2, 0, 256, "w2_a", "w2a_ew")
+        w2_b = load_weight(w2, 256, 512, "w2_b", "w2_b")
+        xw = load_words(x_words, "xw", "xw")
+        price_w = sb.tile([P, TABLE], F32, name="price_w")
+        nc.vector.memset(price_w[:], 0.0)
+        nc.gpsimd.dma_start(price_w[0:1, :], price[0:1, :])
+        ident = sb.tile([P, P], F32, name="ident")
+        make_identity(nc, ident[:])
+        u = sb.tile([P, PACK], F32, name="u")
+        nc.gpsimd.dma_start(u[:], unit.rearrange("(p t) o -> p (t o)", t=PACK))
+
+        xsg = sb.tile([P, S], U8, name="xsg", align_bytes=64)
+        nc.vector.tensor_copy(xsg[:], xs[:].indirect(offs_t[:]))
+        w1_raw = load_weight(w1, 0, 512, "w1_raw", "xs_w1")
+        w2_g = sb.tile([P, 2048], BF16, name="w2_g", align_bytes=64)
+        group_weight(w2_a, w2_g, 0, 64, True)
+        ew = load_words(e_words, "ew", "w2a_ew")
+        group_weight(w2_b, w2_g, 64, P, True)
+        esg = sb.tile([P, E], U8, name="esg", align_bytes=64)
+        nc.vector.tensor_copy(esg[:], es[:].indirect(off_t[:]))
+        w2_q = sb.tile([P, 512], U32, name="w2_q", align_bytes=64)
+        w2_s = early.tile([P, 512], U8, name="w2_s", align_bytes=64, offset=2048)
+        for t in range(PACK):
+            cols = slice(t * P, (t + 1) * P)
+            nc.vector.quantize_mx(out=w2_q[:, cols].bitcast(FP8X4), scales=w2_s[:, cols], in_=w2_g[:, t * 512 : (t + 1) * 512])
+        xg = early.tile([P, S], U32, name="xg", align_bytes=64, offset=0)
+        nc.vector.tensor_copy(xg[:], xw[:].bitcast(U32).indirect(offs_t[:]))
+        yg_ps = []
+        for t in range(PACK):
+            cols = slice(t * P, (t + 1) * P)
+            bank = ps.tile([P, S], F32, name="yg_ps%d" % t, tag="yg%d" % t)
+            nc.tensor.matmul_mx(out=bank[:], lhsT=w2_q[:, cols].bitcast(FP8X4), lhsT_scale=w2_s[:, cols],
+                                rhs=xg[:].bitcast(FP8X4), rhs_scale=xsg[:], start=True, stop=True)
+            yg_ps.append(bank)
+        xsd = sb.tile([P, 2, V], U8, name="xsd", align_bytes=64)
+        nc.vector.tensor_copy(xsd[:].rearrange("p d v -> p v d"), xsg[:].rearrange("p (v d) -> p v d", d=2))
+        xd = sb.tile([P, 2, V], U32, name="xd", align_bytes=64)
+        nc.vector.tensor_copy(xd[:].rearrange("p d v -> p v d"), xg[:].rearrange("p (v d) -> p v d", d=2))
+
+        pg = sb.tile([P, E], F32, name="pg")
+        nc.scalar.activation(pg[:], price_w[:].indirect(off_t[:]), ACT.Copy)
+        pt = ps.tile([P, 4, P], F32, name="pt")
+        for c in range(4):
+            nc.tensor.transpose(pt[:, c, :], pg[:, c * P : (c + 1) * P], ident[:])
+        pcol = sb.tile([P, 4], F32, name="pcol")
+        nc.scalar.copy(pcol[:], pt[:, :, 0])
+        pb = ps.tile([P, E], F32, name="pb")
+        for c in range(4):
+            nc.tensor.transpose(pb[:, c * P : (c + 1) * P], pcol[:, c : c + 1].to_broadcast([P, P]), ident[:])
+        u_sign = sb.tile([P, PACK], F32, name="u_sign")
+        nc.scalar.activation(u_sign[:], u[:], ACT.Sign)
+        u_off = sb.tile([P, PACK], F32, name="u_off")
+        nc.scalar.activation(u_off[:], u[:], ACT.Abs, scale=0.4)
+
+        yg = [sb.tile([P, S], F32, name="yg%d" % t) for t in range(PACK)]
+        g = [sb.tile([P, PACK, V], F32, name="g%d" % h) for h in range(2)]
+
+        def evac_yg(t, on_scalar):
+            if on_scalar:
+                nc.scalar.activation(yg[t][:], yg_ps[t][:], ACT.Copy, scale=0.6)
+            else:
+                nc.vector.tensor_scalar(yg[t][:], yg_ps[t][:], 0.6, None, ALU.mult)
+
+        def gather(dst, window, offsets, on_scalar):
+            if on_scalar:
+                nc.scalar.activation(dst, window.indirect(offsets), ACT.Copy)
+            else:
+                nc.vector.tensor_copy(dst, window.indirect(offsets))
+
+        def gather_sub(t, h, on_scalar):
+            gather(g[h][:, t, :], yg[t][:], sub_t[:, 16 * h : 16 * h + 16], on_scalar)
+
+        for t in range(PACK):
+            evac_yg(t, True)
+            gather_sub(t, 0, t >= 2)
+
+        w1_g = sb.tile([P, 2048], BF16, name="w1_g", align_bytes=64)
+        group_weight(w1_raw, w1_g, 0, P, False)
+        w1_q = sb.tile([P, 512], U32, name="w1_q", align_bytes=64)
+        w1_s = sb.tile([P, 512], U8, name="w1_s", align_bytes=64)
+        nc.vector.quantize_mx(out=w1_q[:].bitcast(FP8X4), scales=w1_s[:], in_=w1_g[:])
+        yp = []
+        for h in range(2):
+            bank = ps.tile([P, PACK, HALF], F32, name="yp%d" % h)
+            vs = slice(h * HALF, (h + 1) * HALF)
+            for t in range(PACK):
+                cols = slice(t * P, (t + 1) * P)
+                for d in range(2):
+                    nc.tensor.matmul_mx(out=bank[:, t, :], lhsT=w1_q[:, cols].bitcast(FP8X4), lhsT_scale=w1_s[:, cols],
+                                        rhs=xd[:, d, vs].bitcast(FP8X4), rhs_scale=xsd[:, d, vs], start=(d == 0), stop=(d == 1))
+            yp.append(bank)
+
+        eg = sb.tile([P, E], U32, name="eg", align_bytes=64)
+
+        def hidden(h):
+            pair = sb.tile([P, PACK * HALF], F32, name="pair%d" % h)
+            bask = sb.tile([P, PACK, HALF], F32, name="bask%d" % h)
+            th = sb.tile([P, PACK, HALF], F32, name="th%d" % h)
+            ab = sb.tile([P, PACK, HALF], F32, name="ab%d" % h)
+            bq = sb.tile([P, PACK, HALF], F32, name="bq%d" % h, tag="bq")
+            hid = sb.tile([P, HALF * PACK], BF16, name="hid%d" % h, tag="hid", align_bytes=64)
+            gv = g[h][:].rearrange("p t (v d) -> p (t v) d", d=2)
+            for a in range(2):
+                cols = slice(a * 256, (a + 1) * 256)
+                nc.vector.tensor_tensor(pair[:, cols], gv[:, cols, 0], gv[:, cols, 1], ALU.add)
+                nc.vector.tensor_tensor(bask[:].rearrange("p t v -> p (t v)")[:, cols], yp[h][:].rearrange("p t v -> p (t v)")[:, cols], pair[:, cols], ALU.add)
+            for t in range(PACK):
+                nc.scalar.activation(th[:, t, :], bask[:, t, :], ACT.Tanh, scale=u_sign[:, t : t + 1])
+                nc.scalar.activation(ab[:, t, :], bask[:, t, :], ACT.Abs, scale=u[:, t : t + 1])
+            for t in range(PACK):
+                nc.vector.scalar_tensor_tensor(bq[:, t, :], ab[:, t, :], u_off[:, t : t + 1], th[:, t, :], ALU.add, ALU.mult)
+            if h == 0:
+                nc.vector.tensor_copy(eg[:], ew[:].bitcast(U32).indirect(off_t[:]))
+            nc.vector.tensor_copy(
+                hid[:].rearrange("p (c i t) -> p c t i", i=4, t=PACK),
+                bq[:].rearrange("p t (c i) -> p c t i", i=4),
+            )
+            hq = sb.tile([P, HALF], U32, name="hq%d" % h, align_bytes=64)
+            hs = sb.tile([P, HALF], U8, name="hs%d" % h, align_bytes=64)
+            nc.vector.quantize_mx(out=hq[:].bitcast(FP8X4), scales=hs[:], in_=hid[:])
+            bank = ps.tile([P, E], F32, name="sc_ps%d" % h, tag="yg%d" % h)
+            nc.tensor.matmul_mx(out=bank[:], lhsT=hq[:].bitcast(FP8X4), lhsT_scale=hs[:],
+                                rhs=eg[:].bitcast(FP8X4), rhs_scale=esg[:], start=True, stop=True)
+            return bank
+
+        def finish(h, sc_ps):
+            half_sc = sb.tile([P, E], F32, name="half_sc%d" % h)
+            nc.scalar.activation(half_sc[:], sc_ps[:], ACT.Copy, scale=0.5)
+            for c in range(2):
+                cols = slice(c * 256, (c + 1) * 256)
+                gc = sb.tile([P, 256], F32, name="gc%d%d" % (h, c))
+                gather(gc[:], half_sc[:], cmp_t[:, 16 * c : 16 * c + 16], (h, c) != (0, 0))
+                own = sb.tile([P, 256], F32, name="own%d%d" % (h, c))
+                nc.vector.scalar_tensor_tensor(own[:], half_sc[:, cols], 1.6, pb[:, cols], ALU.mult, ALU.subtract)
+                r = sb.tile([P, 256], F32, name="r%d%d" % (h, c))
+                nc.vector.tensor_tensor(r[:], gc[:], own[:], ALU.add)
+                o = sb.tile([P, 256], F32, name="o%d%d" % (h, c))
+                nc.vector.scalar_tensor_tensor(o[:], half_sc[:, cols], -0.4, r[:], ALU.mult, ALU.max)
+                nc.sync.dma_start(out[h * HALF : (h + 1) * HALF, cols], o[:])
+
+        sc0 = hidden(0)
+        finish(0, sc0)
+        for t in range(PACK):
+            gather_sub(t, 1, t >= 1)
+        sc1 = hidden(1)
+        finish(1, sc1)

@@ -22,7 +22,7 @@ V = 256
 E = 512
 HALF = 128
 FLOPS = 2 * K * 512 * S * 2 + 2 * 512 * V * E
-M_SCALAR = 40
+M_SCALAR = 32
 
 
 def tile_picked_ybundle_surp_p_kernel(
@@ -40,23 +40,19 @@ def tile_picked_ybundle_surp_p_kernel(
             nc.sync.dma_start(t[:], src)
             return t
 
-        def load_words(src, name, tag):
-            t = sb.tile([P, TABLE], I32, name=name, tag=tag, align_bytes=64)
+        def load_words(src, name, offset):
+            t = early.tile([P, TABLE], I32, name=name, offset=offset, align_bytes=64)
             nc.sync.dma_start(t[:], src[0].rearrange("p n t -> p (n t)").bitcast(I32))
             return t
 
-        def load_scales(t, queues, src):
-            for q in range(4):
-                queues[q].dma_start(t[32 * q : 32 * q + 4, :].bitcast(I32), src[0, 4 * q : 4 * q + 4, :].bitcast(I32))
-
-        def load_weight(src, c0, c1, name, tag):
-            t = sb.tile([P, PACK, c1 - c0], F32, name=name, tag=tag, align_bytes=64)
-            nc.sync.dma_start(t[:], src[:, c0:c1].rearrange("(p j) c -> p j c", j=PACK))
+        def load_weight(src, name, pool, **place):
+            t = pool.tile([P, PACK, 512], F32, name=name, align_bytes=64, **place)
+            nc.sync.dma_start(t[:], src.rearrange("(p j) c -> p j c", j=PACK))
             return t
 
         def group_weight(raw, grouped, m0, m1, on_scalar):
             dst = grouped[:].rearrange("p (t m j) -> p m j t", t=PACK, j=PACK)[:, m0:m1]
-            src = raw[:].rearrange("p j (m t) -> p m j t", t=PACK)
+            src = raw[:].rearrange("p j (m t) -> p m j t", t=PACK)[:, m0:m1]
             if on_scalar:
                 nc.scalar.copy(dst, src)
             else:
@@ -66,48 +62,50 @@ def tile_picked_ybundle_surp_p_kernel(
         off_t = load_list(off, "off_t")
         sub_t = load_list(sub_, "sub_t")
         cmp_t = load_list(cmp, "cmp_t")
-        xs = sb.tile([P, TABLE], U8, name="xs", tag="xs_w1", align_bytes=64)
-        nc.vector.memset(xs[:].bitcast(I32), 0)
-        load_scales(xs, [nc.scalar] * 4, x_scales)
-        es = early.tile([P, TABLE], U8, name="es", align_bytes=64, offset=512)
+        es = early.tile([P, TABLE], U8, name="es", align_bytes=64, offset=0)
         nc.gpsimd.memset(es[:].bitcast(I32), 0)
-        load_scales(es, [nc.scalar, nc.gpsimd, nc.gpsimd, nc.gpsimd], e_scales)
-        w2_a = load_weight(w2, 0, 256, "w2_a", "w2a_ew")
-        w2_b = load_weight(w2, 256, 512, "w2_b", "w2_b")
-        xw = load_words(x_words, "xw", "xw")
+        nc.scalar.dma_start(es[0:16, :].bitcast(I32), e_scales[0].bitcast(I32))
+        xs = early.tile([P, TABLE], U8, name="xs", align_bytes=64, offset=4096)
+        nc.vector.memset(xs[:].bitcast(I32), 0)
+        for q in range(4):
+            nc.scalar.dma_start(xs[32 * q : 32 * q + 4, :].bitcast(I32), x_scales[0, 4 * q : 4 * q + 4, :].bitcast(I32))
+        xw = load_words(x_words, "xw", 16384)
+        w2_raw = load_weight(w2, "w2_raw", sb)
         price_w = sb.tile([P, TABLE], F32, name="price_w")
         nc.vector.memset(price_w[:], 0.0)
-        nc.gpsimd.dma_start(price_w[0:1, :], price[0:1, :])
+        nc.scalar.dma_start(price_w[0:1, :], price[0:1, :])
         ident = sb.tile([P, P], F32, name="ident")
         make_identity(nc, ident[:])
-        u = sb.tile([P, PACK], F32, name="u")
-        nc.gpsimd.dma_start(u[:], unit.rearrange("(p t) o -> p (t o)", t=PACK))
-
-        xsg = sb.tile([P, S], U8, name="xsg", align_bytes=64)
-        nc.vector.tensor_copy(xsg[:], xs[:].indirect(offs_t[:]))
-        w1_raw = load_weight(w1, 0, 512, "w1_raw", "xs_w1")
-        w2_g = sb.tile([P, 2048], BF16, name="w2_g", align_bytes=64)
-        group_weight(w2_a, w2_g, 0, 64, True)
-        ew = load_words(e_words, "ew", "w2a_ew")
-        group_weight(w2_b, w2_g, 64, P, True)
         esg = sb.tile([P, E], U8, name="esg", align_bytes=64)
-        nc.vector.tensor_copy(esg[:], es[:].indirect(off_t[:]))
-        w2_q = sb.tile([P, 512], U32, name="w2_q", align_bytes=64)
-        w2_s = early.tile([P, 512], U8, name="w2_s", align_bytes=64, offset=2048)
-        for t in range(PACK):
-            cols = slice(t * P, (t + 1) * P)
-            nc.vector.quantize_mx(out=w2_q[:, cols].bitcast(FP8X4), scales=w2_s[:, cols], in_=w2_g[:, t * 512 : (t + 1) * 512])
-        xg = early.tile([P, S], U32, name="xg", align_bytes=64, offset=0)
+        nc.gpsimd.memset(esg[:].bitcast(I32), 0)
+
+        es_rows = sb.tile([P, E], U8, name="es_rows", align_bytes=64)
+        nc.vector.tensor_copy(es_rows[:], es[:].indirect(off_t[:]))
+        xsg = early.tile([P, S], U8, name="xsg", align_bytes=64, offset=0)
+        nc.vector.tensor_copy(xsg[:], xs[:].indirect(offs_t[:]))
+        w1_raw = load_weight(w1, "w1_raw", early, offset=4096 + 1024)
+        xsd = sb.tile([P, 2, V], U8, name="xsd", align_bytes=64)
+        nc.vector.tensor_copy(xsd[:].rearrange("p d v -> p v d"), xsg[:].rearrange("p (v d) -> p v d", d=2))
+        xg = early.tile([P, S], U32, name="xg", align_bytes=64, offset=4096 + 512 - 2048)
         nc.vector.tensor_copy(xg[:], xw[:].bitcast(U32).indirect(offs_t[:]))
+        ew = load_words(e_words, "ew", 16384 + 4096)
+        u = early.tile([P, PACK], F32, name="u", align_bytes=64, offset=4096 + 512)
+        nc.sync.dma_start(u[:], unit.rearrange("(p t) o -> p (t o)", t=PACK))
+        for q in range(4):
+            nc.sync.dma_start(esg[32 * q : 32 * q + 4, :].bitcast(I32), es_rows[4 * q : 4 * q + 4, :].bitcast(I32))
+        w2_g = early.tile([P, 2048], BF16, name="w2_g", align_bytes=64, offset=16384)
+        group_weight(w2_raw, w2_g, 0, M_SCALAR, True)
+        group_weight(w2_raw, w2_g, M_SCALAR, P, False)
+        w2_q = sb.tile([P, 512], U32, name="w2_q", align_bytes=64)
+        w2_s = sb.tile([P, 512], U8, name="w2_s", align_bytes=64)
         yg_ps = []
         for t in range(PACK):
             cols = slice(t * P, (t + 1) * P)
+            nc.vector.quantize_mx(out=w2_q[:, cols].bitcast(FP8X4), scales=w2_s[:, cols], in_=w2_g[:, t * 512 : (t + 1) * 512])
             bank = ps.tile([P, S], F32, name="yg_ps%d" % t, tag="yg%d" % t)
             nc.tensor.matmul_mx(out=bank[:], lhsT=w2_q[:, cols].bitcast(FP8X4), lhsT_scale=w2_s[:, cols],
                                 rhs=xg[:].bitcast(FP8X4), rhs_scale=xsg[:], start=True, stop=True)
             yg_ps.append(bank)
-        xsd = sb.tile([P, 2, V], U8, name="xsd", align_bytes=64)
-        nc.vector.tensor_copy(xsd[:].rearrange("p d v -> p v d"), xsg[:].rearrange("p (v d) -> p v d", d=2))
         xd = sb.tile([P, 2, V], U32, name="xd", align_bytes=64)
         nc.vector.tensor_copy(xd[:].rearrange("p d v -> p v d"), xg[:].rearrange("p (v d) -> p v d", d=2))
 

@@ -22,7 +22,7 @@ V = 256
 E = 512
 HALF = 128
 FLOPS = 2 * K * 512 * S * 2 + 2 * 512 * V * E
-M_SCALAR = 32
+M_SCALAR = 64
 
 
 def tile_picked_ybundle_surp_p_kernel(
@@ -51,53 +51,60 @@ def tile_picked_ybundle_surp_p_kernel(
             return t
 
         def group_weight(raw, grouped, m0, m1, on_scalar):
-            dst = grouped[:].rearrange("p (t m j) -> p m j t", t=PACK, j=PACK)[:, m0:m1]
-            src = raw[:].rearrange("p j (m t) -> p m j t", t=PACK)[:, m0:m1]
+            dst = grouped[:].rearrange("p (t m j) -> p m t j", t=PACK, j=PACK)[:, m0:m1]
+            src = raw[:].rearrange("p j (m t) -> p m t j", t=PACK)[:, m0:m1]
             if on_scalar:
                 nc.scalar.copy(dst, src)
             else:
                 nc.vector.tensor_copy(dst, src)
 
-        offs_t = load_list(offs, "offs_t")
-        off_t = load_list(off, "off_t")
-        sub_t = load_list(sub_, "sub_t")
-        cmp_t = load_list(cmp, "cmp_t")
-        es = early.tile([P, TABLE], U8, name="es", align_bytes=64, offset=0)
-        nc.gpsimd.memset(es[:].bitcast(I32), 0)
-        nc.scalar.dma_start(es[0:16, :].bitcast(I32), e_scales[0].bitcast(I32))
-        xs = early.tile([P, TABLE], U8, name="xs", align_bytes=64, offset=4096)
-        nc.vector.memset(xs[:].bitcast(I32), 0)
-        for q in range(4):
-            nc.scalar.dma_start(xs[32 * q : 32 * q + 4, :].bitcast(I32), x_scales[0, 4 * q : 4 * q + 4, :].bitcast(I32))
-        xw = load_words(x_words, "xw", 16384)
-        w2_raw = load_weight(w2, "w2_raw", sb)
+        def load_scale_rows(src, name, offset, clear):
+            t = early.tile([P, TABLE], U8, name=name, align_bytes=64, offset=offset)
+            for half in range(2):
+                nc.sync.dma_start(t[16 * half : 16 * half + 16, :].bitcast(I32), src[0].bitcast(I32))
+            clear.memset(t[32:64, :].bitcast(I32), 0)
+            clear.memset(t[64:128, :].bitcast(I32), 0)
+            return t
+
         price_w = sb.tile([P, TABLE], F32, name="price_w")
         nc.vector.memset(price_w[:], 0.0)
-        nc.scalar.dma_start(price_w[0:1, :], price[0:1, :])
-        ident = sb.tile([P, P], F32, name="ident")
-        make_identity(nc, ident[:])
+        offs_t = load_list(offs, "offs_t")
+        xs = load_scale_rows(x_scales, "xs", 4096, nc.gpsimd)
+        off_t = load_list(off, "off_t")
+        w2_raw = load_weight(w2, "w2_raw", sb)
+        es = load_scale_rows(e_scales, "es", 0, nc.vector)
+        sub_t = load_list(sub_, "sub_t")
+        cmp_t = load_list(cmp, "cmp_t")
+        nc.sync.dma_start(price_w[0:1, :], price[0:1, :])
+        xw = load_words(x_words, "xw", 16384)
+        xsg = sb.tile([P, S], U8, name="xsg", align_bytes=64)
+        nc.gpsimd.memset(xsg[:].bitcast(I32), 0)
         esg = sb.tile([P, E], U8, name="esg", align_bytes=64)
         nc.gpsimd.memset(esg[:].bitcast(I32), 0)
+        ident = sb.tile([P, P], F32, name="ident")
+        make_identity(nc, ident[:])
 
+        def place_scales(plane, rows):
+            for q in range(4):
+                nc.sync.dma_start(plane[32 * q : 32 * q + 4, :].bitcast(I32), rows[4 * q : 4 * q + 4, :].bitcast(I32))
+
+        xs_rows = sb.tile([P, S], U8, name="xs_rows", align_bytes=64)
+        nc.vector.tensor_copy(xs_rows[:], xs[:].indirect(offs_t[:]))
+        place_scales(xsg, xs_rows)
+        w1_raw = load_weight(w1, "w1_raw", early, offset=4096 + 1024)
+        u = early.tile([P, PACK], F32, name="u", align_bytes=64, offset=4096 + 512)
+        nc.sync.dma_start(u[:], unit.rearrange("(p t) o -> p (t o)", t=PACK))
+        w2_g = sb.tile([P, 2048], BF16, name="w2_g", align_bytes=64)
+        group_weight(w2_raw, w2_g, 0, M_SCALAR, True)
+        group_weight(w2_raw, w2_g, M_SCALAR, P, False)
         es_rows = sb.tile([P, E], U8, name="es_rows", align_bytes=64)
         nc.vector.tensor_copy(es_rows[:], es[:].indirect(off_t[:]))
-        xsg = early.tile([P, S], U8, name="xsg", align_bytes=64, offset=0)
-        nc.vector.tensor_copy(xsg[:], xs[:].indirect(offs_t[:]))
-        w1_raw = load_weight(w1, "w1_raw", early, offset=4096 + 1024)
-        xsd = sb.tile([P, 2, V], U8, name="xsd", align_bytes=64)
-        nc.vector.tensor_copy(xsd[:].rearrange("p d v -> p v d"), xsg[:].rearrange("p (v d) -> p v d", d=2))
+        w2_q = sb.tile([P, 512], U32, name="w2_q", align_bytes=64)
+        w2_s = sb.tile([P, 512], U8, name="w2_s", align_bytes=64)
         xg = early.tile([P, S], U32, name="xg", align_bytes=64, offset=4096 + 512 - 2048)
         nc.vector.tensor_copy(xg[:], xw[:].bitcast(U32).indirect(offs_t[:]))
         ew = load_words(e_words, "ew", 16384 + 4096)
-        u = early.tile([P, PACK], F32, name="u", align_bytes=64, offset=4096 + 512)
-        nc.sync.dma_start(u[:], unit.rearrange("(p t) o -> p (t o)", t=PACK))
-        for q in range(4):
-            nc.sync.dma_start(esg[32 * q : 32 * q + 4, :].bitcast(I32), es_rows[4 * q : 4 * q + 4, :].bitcast(I32))
-        w2_g = early.tile([P, 2048], BF16, name="w2_g", align_bytes=64, offset=16384)
-        group_weight(w2_raw, w2_g, 0, M_SCALAR, True)
-        group_weight(w2_raw, w2_g, M_SCALAR, P, False)
-        w2_q = sb.tile([P, 512], U32, name="w2_q", align_bytes=64)
-        w2_s = sb.tile([P, 512], U8, name="w2_s", align_bytes=64)
+        place_scales(esg, es_rows)
         yg_ps = []
         for t in range(PACK):
             cols = slice(t * P, (t + 1) * P)
@@ -107,7 +114,9 @@ def tile_picked_ybundle_surp_p_kernel(
                                 rhs=xg[:].bitcast(FP8X4), rhs_scale=xsg[:], start=True, stop=True)
             yg_ps.append(bank)
         xd = sb.tile([P, 2, V], U32, name="xd", align_bytes=64)
-        nc.vector.tensor_copy(xd[:].rearrange("p d v -> p v d"), xg[:].rearrange("p (v d) -> p v d", d=2))
+        nc.vector.tensor_copy(xd[:], xg[:].rearrange("p (v d) -> p d v", d=2))
+        xsd = sb.tile([P, 2, V], U8, name="xsd", align_bytes=64)
+        nc.vector.tensor_copy(xsd[:], xsg[:].rearrange("p (v d) -> p d v", d=2))
 
         pg = sb.tile([P, E], F32, name="pg")
         nc.scalar.activation(pg[:], price_w[:].indirect(off_t[:]), ACT.Copy)
@@ -125,7 +134,7 @@ def tile_picked_ybundle_surp_p_kernel(
         nc.scalar.activation(u_off[:], u[:], ACT.Abs, scale=0.4)
 
         yg = [sb.tile([P, S], F32, name="yg%d" % t) for t in range(PACK)]
-        g = [sb.tile([P, PACK, V], F32, name="g%d" % h) for h in range(2)]
+        g = [[sb.tile([P, 2, V], F32, name="g%d%d" % (h, a)) for a in range(2)] for h in range(2)]
 
         def evac_yg(t, on_scalar):
             if on_scalar:
@@ -140,52 +149,52 @@ def tile_picked_ybundle_surp_p_kernel(
                 nc.vector.tensor_copy(dst, window.indirect(offsets))
 
         def gather_sub(t, h, on_scalar):
-            gather(g[h][:, t, :], yg[t][:], sub_t[:, 16 * h : 16 * h + 16], on_scalar)
+            gather(g[h][t // 2][:, t % 2, :], yg[t][:], sub_t[:, 16 * h : 16 * h + 16], on_scalar)
 
-        for t in range(PACK):
-            evac_yg(t, True)
-            gather_sub(t, 0, t >= 2)
-
-        w1_g = sb.tile([P, 2048], BF16, name="w1_g", align_bytes=64)
+        w1_g = early.tile([P, 2048], BF16, name="w1_g", align_bytes=64, offset=32768)
         group_weight(w1_raw, w1_g, 0, P, False)
         w1_q = sb.tile([P, 512], U32, name="w1_q", align_bytes=64)
         w1_s = sb.tile([P, 512], U8, name="w1_s", align_bytes=64)
-        nc.vector.quantize_mx(out=w1_q[:].bitcast(FP8X4), scales=w1_s[:], in_=w1_g[:])
         yp = []
-        for h in range(2):
-            bank = ps.tile([P, PACK, HALF], F32, name="yp%d" % h)
-            vs = slice(h * HALF, (h + 1) * HALF)
-            for t in range(PACK):
+        for a in range(2):
+            nc.vector.quantize_mx(out=w1_q[:, a * 256 : (a + 1) * 256].bitcast(FP8X4), scales=w1_s[:, a * 256 : (a + 1) * 256], in_=w1_g[:, a * 1024 : (a + 1) * 1024])
+            bank = ps.tile([P, 2, V], F32, name="yp%d" % a)
+            for t in range(2 * a, 2 * a + 2):
                 cols = slice(t * P, (t + 1) * P)
                 for d in range(2):
-                    nc.tensor.matmul_mx(out=bank[:, t, :], lhsT=w1_q[:, cols].bitcast(FP8X4), lhsT_scale=w1_s[:, cols],
-                                        rhs=xd[:, d, vs].bitcast(FP8X4), rhs_scale=xsd[:, d, vs], start=(d == 0), stop=(d == 1))
+                    nc.tensor.matmul_mx(out=bank[:, t % 2, :], lhsT=w1_q[:, cols].bitcast(FP8X4), lhsT_scale=w1_s[:, cols],
+                                        rhs=xd[:, d, :].bitcast(FP8X4), rhs_scale=xsd[:, d, :], start=(d == 0), stop=(d == 1))
             yp.append(bank)
 
+        for t in range(PACK):
+            evac_yg(t, t != 1)
+            gather_sub(t, 0, t >= 2)
+
         eg = sb.tile([P, E], U32, name="eg", align_bytes=64)
+        nc.vector.tensor_copy(eg[:], ew[:].bitcast(U32).indirect(off_t[:]))
 
         def hidden(h):
-            pair = sb.tile([P, PACK * HALF], F32, name="pair%d" % h)
-            bask = sb.tile([P, PACK, HALF], F32, name="bask%d" % h)
             th = sb.tile([P, PACK, HALF], F32, name="th%d" % h)
             ab = sb.tile([P, PACK, HALF], F32, name="ab%d" % h)
-            bq = sb.tile([P, PACK, HALF], F32, name="bq%d" % h, tag="bq")
+            bq = sb.tile([P, PACK, HALF], F32, name="bq%d" % h)
             hid = sb.tile([P, HALF * PACK], BF16, name="hid%d" % h, tag="hid", align_bytes=64)
-            gv = g[h][:].rearrange("p t (v d) -> p (t v) d", d=2)
+            bask = []
             for a in range(2):
-                cols = slice(a * 256, (a + 1) * 256)
-                nc.vector.tensor_tensor(pair[:, cols], gv[:, cols, 0], gv[:, cols, 1], ALU.add)
-                nc.vector.tensor_tensor(bask[:].rearrange("p t v -> p (t v)")[:, cols], yp[h][:].rearrange("p t v -> p (t v)")[:, cols], pair[:, cols], ALU.add)
+                pair = early.tile([P, 2, HALF], F32, name="pair%d%d" % (h, a), align_bytes=64, offset=32768 + 1536 + 1024 * a)
+                gv = g[h][a][:].rearrange("p t (v d) -> p (t v) d", d=2)
+                nc.vector.tensor_tensor(pair[:].rearrange("p t v -> p (t v)"), gv[:, :, 0], gv[:, :, 1], ALU.add)
+                b = sb.tile([P, 2, HALF], F32, name="bask%d%d" % (h, a), tag="bask%d" % a)
+                nc.vector.tensor_tensor(b[:], yp[a][:, :, h * HALF : (h + 1) * HALF], pair[:], ALU.add)
+                bask.append(b)
             for t in range(PACK):
-                nc.scalar.activation(th[:, t, :], bask[:, t, :], ACT.Tanh, scale=u_sign[:, t : t + 1])
-                nc.scalar.activation(ab[:, t, :], bask[:, t, :], ACT.Abs, scale=u[:, t : t + 1])
+                b = bask[t // 2][:, t % 2, :]
+                nc.scalar.activation(th[:, t, :], b, ACT.Tanh, scale=u_sign[:, t : t + 1])
+                nc.scalar.activation(ab[:, t, :], b, ACT.Abs, scale=u[:, t : t + 1])
             for t in range(PACK):
                 nc.vector.scalar_tensor_tensor(bq[:, t, :], ab[:, t, :], u_off[:, t : t + 1], th[:, t, :], ALU.add, ALU.mult)
-            if h == 0:
-                nc.vector.tensor_copy(eg[:], ew[:].bitcast(U32).indirect(off_t[:]))
             nc.vector.tensor_copy(
-                hid[:].rearrange("p (c i t) -> p c t i", i=4, t=PACK),
-                bq[:].rearrange("p t (c i) -> p c t i", i=4),
+                hid[:].rearrange("p (v t) -> p v t", t=PACK),
+                bq[:].rearrange("p t v -> p v t"),
             )
             hq = sb.tile([P, HALF], U32, name="hq%d" % h, align_bytes=64)
             hs = sb.tile([P, HALF], U8, name="hs%d" % h, align_bytes=64)
@@ -211,8 +220,8 @@ def tile_picked_ybundle_surp_p_kernel(
                 nc.sync.dma_start(out[h * HALF : (h + 1) * HALF, cols], o[:])
 
         sc0 = hidden(0)
-        finish(0, sc0)
         for t in range(PACK):
-            gather_sub(t, 1, t >= 1)
+            gather_sub(t, 1, True)
         sc1 = hidden(1)
+        finish(0, sc0)
         finish(1, sc1)

@@ -69,7 +69,7 @@ def tile_picked_ybundle_surp_p_kernel(
         price_w = sb.tile([P, TABLE], F32, name="price_w")
         nc.vector.memset(price_w[:], 0.0)
         offs_t = load_list(offs, "offs_t")
-        xs = load_scale_rows(x_scales, "xs", 4096, nc.gpsimd)
+        xs = load_scale_rows(x_scales, "xs", 4096, nc.vector)
         off_t = load_list(off, "off_t")
         w2_raw = load_weight(w2, "w2_raw", sb)
         es = load_scale_rows(e_scales, "es", 0, nc.vector)
@@ -128,13 +128,16 @@ def tile_picked_ybundle_surp_p_kernel(
         pb = ps.tile([P, E], F32, name="pb")
         for c in range(4):
             nc.tensor.transpose(pb[:, c * P : (c + 1) * P], pcol[:, c : c + 1].to_broadcast([P, P]), ident[:])
+        pr = sb.tile([P, E], F32, name="pr")
+        nc.scalar.copy(pr[:], pb[:])
         u_sign = sb.tile([P, PACK], F32, name="u_sign")
         nc.scalar.activation(u_sign[:], u[:], ACT.Sign)
         u_off = sb.tile([P, PACK], F32, name="u_off")
         nc.scalar.activation(u_off[:], u[:], ACT.Abs, scale=0.4)
 
         yg = [sb.tile([P, S], F32, name="yg%d" % t) for t in range(PACK)]
-        g = [[sb.tile([P, 2, V], F32, name="g%d%d" % (h, a)) for a in range(2)] for h in range(2)]
+        g = [[early.tile([P, 2, V], F32, name="g%d%d" % (h, a), align_bytes=64, offset=5120 + 2048 * (2 * h + a)) for a in range(2)]
+             for h in range(2)]
 
         def evac_yg(t, on_scalar):
             if on_scalar:
@@ -167,16 +170,16 @@ def tile_picked_ybundle_surp_p_kernel(
             yp.append(bank)
 
         for t in range(PACK):
-            evac_yg(t, t != 1)
+            evac_yg(t, True)
             gather_sub(t, 0, t >= 2)
 
         eg = sb.tile([P, E], U32, name="eg", align_bytes=64)
         nc.vector.tensor_copy(eg[:], ew[:].bitcast(U32).indirect(off_t[:]))
 
         def hidden(h):
-            th = sb.tile([P, PACK, HALF], F32, name="th%d" % h)
-            ab = sb.tile([P, PACK, HALF], F32, name="ab%d" % h)
-            bq = sb.tile([P, PACK, HALF], F32, name="bq%d" % h)
+            th = [sb.tile([P, HALF], F32, name="th%d%d" % (h, t), tag="th%d" % t) for t in range(PACK)]
+            ab = [sb.tile([P, HALF], F32, name="ab%d%d" % (h, t), tag="ab%d" % t) for t in range(PACK)]
+            bq = sb.tile([P, PACK, HALF], F32, name="bq%d" % h, tag="bq")
             hid = sb.tile([P, HALF * PACK], BF16, name="hid%d" % h, tag="hid", align_bytes=64)
             bask = []
             for a in range(2):
@@ -188,10 +191,10 @@ def tile_picked_ybundle_surp_p_kernel(
                 bask.append(b)
             for t in range(PACK):
                 b = bask[t // 2][:, t % 2, :]
-                nc.scalar.activation(th[:, t, :], b, ACT.Tanh, scale=u_sign[:, t : t + 1])
-                nc.scalar.activation(ab[:, t, :], b, ACT.Abs, scale=u[:, t : t + 1])
+                nc.scalar.activation(th[t][:], b, ACT.Tanh, scale=u_sign[:, t : t + 1])
+                nc.scalar.activation(ab[t][:], b, ACT.Abs, scale=u[:, t : t + 1])
             for t in range(PACK):
-                nc.vector.scalar_tensor_tensor(bq[:, t, :], ab[:, t, :], u_off[:, t : t + 1], th[:, t, :], ALU.add, ALU.mult)
+                nc.vector.scalar_tensor_tensor(bq[:, t, :], ab[t][:], u_off[:, t : t + 1], th[t][:], ALU.add, ALU.mult)
             nc.vector.tensor_copy(
                 hid[:].rearrange("p (v t) -> p v t", t=PACK),
                 bq[:].rearrange("p t v -> p v t"),
@@ -207,21 +210,24 @@ def tile_picked_ybundle_surp_p_kernel(
         def finish(h, sc_ps):
             half_sc = sb.tile([P, E], F32, name="half_sc%d" % h)
             nc.scalar.activation(half_sc[:], sc_ps[:], ACT.Copy, scale=0.5)
-            for c in range(2):
-                cols = slice(c * 256, (c + 1) * 256)
-                gc = sb.tile([P, 256], F32, name="gc%d%d" % (h, c))
-                gather(gc[:], half_sc[:], cmp_t[:, 16 * c : 16 * c + 16], (h, c) != (0, 0))
-                own = sb.tile([P, 256], F32, name="own%d%d" % (h, c))
-                nc.vector.scalar_tensor_tensor(own[:], half_sc[:, cols], 1.6, pb[:, cols], ALU.mult, ALU.subtract)
-                r = sb.tile([P, 256], F32, name="r%d%d" % (h, c))
-                nc.vector.tensor_tensor(r[:], gc[:], own[:], ALU.add)
+            lo, hi = slice(0, 256), slice(256, 512)
+            d_lo = sb.tile([P, 256], F32, name="d_lo%d" % h)
+            nc.vector.tensor_tensor(d_lo[:], half_sc[:].indirect(cmp_t[:, 0:16]), pr[:, lo], ALU.subtract)
+            g_hi = sb.tile([P, 256], F32, name="g_hi%d" % h)
+            nc.scalar.activation(g_hi[:], half_sc[:].indirect(cmp_t[:, 16:32]), ACT.Copy)
+            own_hi = sb.tile([P, 256], F32, name="own_hi%d" % h)
+            nc.vector.scalar_tensor_tensor(own_hi[:], half_sc[:, hi], 1.6, pr[:, hi], ALU.mult, ALU.subtract)
+            r = sb.tile([P, E], F32, name="r%d" % h)
+            nc.vector.scalar_tensor_tensor(r[:, lo], half_sc[:, lo], 1.6, d_lo[:], ALU.mult, ALU.add)
+            nc.vector.tensor_tensor(r[:, hi], g_hi[:], own_hi[:], ALU.add)
+            for c, cols in enumerate((lo, hi)):
                 o = sb.tile([P, 256], F32, name="o%d%d" % (h, c))
-                nc.vector.scalar_tensor_tensor(o[:], half_sc[:, cols], -0.4, r[:], ALU.mult, ALU.max)
+                nc.vector.scalar_tensor_tensor(o[:], half_sc[:, cols], -0.4, r[:, cols], ALU.mult, ALU.max)
                 nc.sync.dma_start(out[h * HALF : (h + 1) * HALF, cols], o[:])
 
         sc0 = hidden(0)
         for t in range(PACK):
-            gather_sub(t, 1, True)
+            gather_sub(t, 1, t >= 1)
         sc1 = hidden(1)
         finish(0, sc0)
         finish(1, sc1)

from contextlib import ExitStack

import concourse.mybir as mybir
from concourse.masks import make_identity

F32 = mybir.dt.float32
BF16 = mybir.dt.bfloat16
I32 = mybir.dt.int32
U32 = mybir.dt.uint32
U16 = mybir.dt.uint16
U8 = mybir.dt.uint8
FP8X4 = mybir.dt.float8_e4m3fn_x4
ALU = mybir.AluOpType
ACT = mybir.ActivationFunctionType

P = 128
PACK = 4
K = 512
TABLE = 2048
S = 512
V = 256
E = 512
HALF = 128
FLOPS = 2 * K * 512 * S * 2 + 2 * 512 * V * E
M_SCALAR = 64


def tile_picked_ybundle_surp_p_kernel(
    tc, x_words, x_scales, w1, w2, e_words, e_scales, unit, price, offs, sub_, off, cmp, out
):
    nc = tc.nc
    with ExitStack() as ctx:
        lists = ctx.enter_context(tc.tile_pool(name="lists", bufs=1))
        sb = ctx.enter_context(tc.tile_pool(name="sb", bufs=1))
        early = ctx.enter_context(tc.tile_pool(name="early", bufs=1))
        ps = ctx.enter_context(tc.psum_pool(name="ps", bufs=1))

        def load_list(src, name):
            t = lists.tile([P, 32], U16, name=name)
            nc.sync.dma_start(t[:], src)
            return t

        def load_words(src, name, offset):
            t = early.tile([P, TABLE], I32, name=name, offset=offset, align_bytes=64)
            nc.sync.dma_start(t[:], src[0].rearrange("p n t -> p (n t)").bitcast(I32))
            return t

        def load_weight(src, name, pool, **place):
            t = pool.tile([P, PACK, 512], F32, name=name, align_bytes=64, **place)
            nc.sync.dma_start(t[:], src.rearrange("(p j) c -> p j c", j=PACK))
            return t

        def group_weight(raw, grouped, m0, m1, on_scalar):
            dst = grouped[:].rearrange("p (t m j) -> p m t j", t=PACK, j=PACK)[:, m0:m1]
            src = raw[:].rearrange("p j (m t) -> p m t j", t=PACK)[:, m0:m1]
            if on_scalar:
                nc.scalar.copy(dst, src)
            else:
                nc.vector.tensor_copy(dst, src)

        def load_scale_rows(src, name, offset, clear):
            t = early.tile([P, TABLE], U8, name=name, align_bytes=64, offset=offset)
            for half in range(2):
                nc.sync.dma_start(t[16 * half : 16 * half + 16, :].bitcast(I32), src[0].bitcast(I32))
            clear.memset(t[32:64, :].bitcast(I32), 0)
            clear.memset(t[64:128, :].bitcast(I32), 0)
            return t

        price_w = sb.tile([P, TABLE], F32, name="price_w")
        nc.vector.memset(price_w[:], 0.0)
        offs_t = load_list(offs, "offs_t")
        xs = load_scale_rows(x_scales, "xs", 4096, nc.vector)
        off_t = load_list(off, "off_t")
        w2_raw = load_weight(w2, "w2_raw", sb)
        es = load_scale_rows(e_scales, "es", 0, nc.vector)
        sub_t = load_list(sub_, "sub_t")
        cmp_t = load_list(cmp, "cmp_t")
        nc.sync.dma_start(price_w[0:1, :], price[0:1, :])
        xw = load_words(x_words, "xw", 16384)
        xsg = sb.tile([P, S], U8, name="xsg", align_bytes=64)
        nc.gpsimd.memset(xsg[:].bitcast(I32), 0)
        esg = sb.tile([P, E], U8, name="esg", align_bytes=64)
        nc.gpsimd.memset(esg[:].bitcast(I32), 0)
        ident = sb.tile([P, P], F32, name="ident")
        make_identity(nc, ident[:])

        def place_scales(plane, rows):
            for q in range(4):
                nc.sync.dma_start(plane[32 * q : 32 * q + 4, :].bitcast(I32), rows[4 * q : 4 * q + 4, :].bitcast(I32))

        xs_rows = sb.tile([P, S], U8, name="xs_rows", align_bytes=64)
        nc.vector.tensor_copy(xs_rows[:], xs[:].indirect(offs_t[:]))
        place_scales(xsg, xs_rows)
        w1_raw = load_weight(w1, "w1_raw", early, offset=4096 + 1024)
        u = early.tile([P, PACK], F32, name="u", align_bytes=64, offset=4096 + 512)
        nc.sync.dma_start(u[:], unit.rearrange("(p t) o -> p (t o)", t=PACK))
        w2_g = sb.tile([P, 2048], BF16, name="w2_g", align_bytes=64)
        group_weight(w2_raw, w2_g, 0, M_SCALAR, True)
        group_weight(w2_raw, w2_g, M_SCALAR, P, False)
        es_rows = sb.tile([P, E], U8, name="es_rows", align_bytes=64)
        nc.vector.tensor_copy(es_rows[:], es[:].indirect(off_t[:]))
        w2_q = sb.tile([P, 512], U32, name="w2_q", align_bytes=64)
        w2_s = sb.tile([P, 512], U8, name="w2_s", align_bytes=64)
        xg = early.tile([P, S], U32, name="xg", align_bytes=64, offset=4096 + 512 - 2048)
        nc.vector.tensor_copy(xg[:], xw[:].bitcast(U32).indirect(offs_t[:]))
        ew = load_words(e_words, "ew", 16384 + 4096)
        place_scales(esg, es_rows)
        yg_ps = []
        for t in range(PACK):
            cols = slice(t * P, (t + 1) * P)
            nc.vector.quantize_mx(out=w2_q[:, cols].bitcast(FP8X4), scales=w2_s[:, cols], in_=w2_g[:, t * 512 : (t + 1) * 512])
            bank = ps.tile([P, S], F32, name="yg_ps%d" % t, tag="yg%d" % t)
            nc.tensor.matmul_mx(out=bank[:], lhsT=w2_q[:, cols].bitcast(FP8X4), lhsT_scale=w2_s[:, cols],
                                rhs=xg[:].bitcast(FP8X4), rhs_scale=xsg[:], start=True, stop=True)
            yg_ps.append(bank)
        xd = sb.tile([P, 2, V], U32, name="xd", align_bytes=64)
        nc.vector.tensor_copy(xd[:], xg[:].rearrange("p (v d) -> p d v", d=2))
        xsd = sb.tile([P, 2, V], U8, name="xsd", align_bytes=64)
        nc.vector.tensor_copy(xsd[:], xsg[:].rearrange("p (v d) -> p d v", d=2))

        pg = sb.tile([P, E], F32, name="pg")
        nc.scalar.activation(pg[:], price_w[:].indirect(off_t[:]), ACT.Copy)
        pt = ps.tile([P, 4, P], F32, name="pt")
        for c in range(4):
            nc.tensor.transpose(pt[:, c, :], pg[:, c * P : (c + 1) * P], ident[:])
        pcol = sb.tile([P, 4], F32, name="pcol")
        nc.scalar.copy(pcol[:], pt[:, :, 0])
        pb = ps.tile([P, E], F32, name="pb")
        for c in range(4):
            nc.tensor.transpose(pb[:, c * P : (c + 1) * P], pcol[:, c : c + 1].to_broadcast([P, P]), ident[:])
        pr = sb.tile([P, E], F32, name="pr")
        nc.scalar.copy(pr[:], pb[:])
        u_sign = sb.tile([P, PACK], F32, name="u_sign")
        nc.scalar.activation(u_sign[:], u[:], ACT.Sign)
        u_off = sb.tile([P, PACK], F32, name="u_off")
        nc.scalar.activation(u_off[:], u[:], ACT.Abs, scale=0.4)

        yg = [sb.tile([P, S], F32, name="yg%d" % t) for t in range(PACK)]
        g = [[early.tile([P, 2, V], F32, name="g%d%d" % (h, a), align_bytes=64, offset=5120 + 2048 * (2 * h + a)) for a in range(2)]
             for h in range(2)]

        def evac_yg(t, on_scalar):
            if on_scalar:
                nc.scalar.activation(yg[t][:], yg_ps[t][:], ACT.Copy, scale=0.6)
            else:
                nc.vector.tensor_scalar(yg[t][:], yg_ps[t][:], 0.6, None, ALU.mult)

        def gather(dst, window, offsets, on_scalar):
            if on_scalar:
                nc.scalar.activation(dst, window.indirect(offsets), ACT.Copy)
            else:
                nc.vector.tensor_copy(dst, window.indirect(offsets))

        def gather_sub(t, h, on_scalar):
            gather(g[h][t // 2][:, t % 2, :], yg[t][:], sub_t[:, 16 * h : 16 * h + 16], on_scalar)

        w1_g = early.tile([P, 2048], BF16, name="w1_g", align_bytes=64, offset=32768)
        group_weight(w1_raw, w1_g, 0, P, False)
        w1_q = sb.tile([P, 512], U32, name="w1_q", align_bytes=64)
        w1_s = sb.tile([P, 512], U8, name="w1_s", align_bytes=64)
        yp = []
        for a in range(2):
            nc.vector.quantize_mx(out=w1_q[:, a * 256 : (a + 1) * 256].bitcast(FP8X4), scales=w1_s[:, a * 256 : (a + 1) * 256], in_=w1_g[:, a * 1024 : (a + 1) * 1024])
            bank = ps.tile([P, 2, V], F32, name="yp%d" % a)
            for t in range(2 * a, 2 * a + 2):
                cols = slice(t * P, (t + 1) * P)
                for d in range(2):
                    nc.tensor.matmul_mx(out=bank[:, t % 2, :], lhsT=w1_q[:, cols].bitcast(FP8X4), lhsT_scale=w1_s[:, cols],
                                        rhs=xd[:, d, :].bitcast(FP8X4), rhs_scale=xsd[:, d, :], start=(d == 0), stop=(d == 1))
            yp.append(bank)

        for t in range(PACK):
            evac_yg(t, True)
            gather_sub(t, 0, t >= 2)

        eg = sb.tile([P, E], U32, name="eg", align_bytes=64)
        nc.vector.tensor_copy(eg[:], ew[:].bitcast(U32).indirect(off_t[:]))

        def hidden(h):
            th = [sb.tile([P, HALF], F32, name="th%d%d" % (h, t), tag="th%d" % t) for t in range(PACK)]
            ab = [sb.tile([P, HALF], F32, name="ab%d%d" % (h, t), tag="ab%d" % t) for t in range(PACK)]
            bq = sb.tile([P, PACK, HALF], F32, name="bq%d" % h, tag="bq")
            hid = sb.tile([P, HALF * PACK], BF16, name="hid%d" % h, tag="hid", align_bytes=64)
            bask = []
            for a in range(2):
                pair = early.tile([P, 2, HALF], F32, name="pair%d%d" % (h, a), align_bytes=64, offset=32768 + 1536 + 1024 * a)
                gv = g[h][a][:].rearrange("p t (v d) -> p (t v) d", d=2)
                nc.vector.tensor_tensor(pair[:].rearrange("p t v -> p (t v)"), gv[:, :, 0], gv[:, :, 1], ALU.add)
                b = sb.tile([P, 2, HALF], F32, name="bask%d%d" % (h, a), tag="bask%d" % a)
                nc.vector.tensor_tensor(b[:], yp[a][:, :, h * HALF : (h + 1) * HALF], pair[:], ALU.add)
                bask.append(b)
            for t in range(PACK):
                b = bask[t // 2][:, t % 2, :]
                nc.scalar.activation(th[t][:], b, ACT.Tanh, scale=u_sign[:, t : t + 1])
                nc.scalar.activation(ab[t][:], b, ACT.Abs, scale=u[:, t : t + 1])
            for t in range(PACK):
                nc.vector.scalar_tensor_tensor(bq[:, t, :], ab[t][:], u_off[:, t : t + 1], th[t][:], ALU.add, ALU.mult)
            nc.vector.tensor_copy(
                hid[:].rearrange("p (v t) -> p v t", t=PACK),
                bq[:].rearrange("p t v -> p v t"),
            )
            hq = sb.tile([P, HALF], U32, name="hq%d" % h, align_bytes=64)
            hs = sb.tile([P, HALF], U8, name="hs%d" % h, align_bytes=64)
            nc.vector.quantize_mx(out=hq[:].bitcast(FP8X4), scales=hs[:], in_=hid[:])
            bank = ps.tile([P, E], F32, name="sc_ps%d" % h, tag="yg%d" % h)
            nc.tensor.matmul_mx(out=bank[:], lhsT=hq[:].bitcast(FP8X4), lhsT_scale=hs[:],
                                rhs=eg[:].bitcast(FP8X4), rhs_scale=esg[:], start=True, stop=True)
            return bank

        def finish(h, sc_ps):
            half_sc = sb.tile([P, E], F32, name="half_sc%d" % h)
            nc.scalar.activation(half_sc[:], sc_ps[:], ACT.Copy, scale=0.5)
            lo, hi = slice(0, 256), slice(256, 512)
            d_lo = sb.tile([P, 256], F32, name="d_lo%d" % h)
            nc.vector.tensor_tensor(d_lo[:], half_sc[:].indirect(cmp_t[:, 0:16]), pr[:, lo], ALU.subtract)
            g_hi = sb.tile([P, 256], F32, name="g_hi%d" % h)
            nc.scalar.activation(g_hi[:], half_sc[:].indirect(cmp_t[:, 16:32]), ACT.Copy)
            own_hi = sb.tile([P, 256], F32, name="own_hi%d" % h)
            nc.vector.scalar_tensor_tensor(own_hi[:], half_sc[:, hi], 1.6, pr[:, hi], ALU.mult, ALU.subtract)
            r = sb.tile([P, E], F32, name="r%d" % h)
            nc.vector.scalar_tensor_tensor(r[:, lo], half_sc[:, lo], 1.6, d_lo[:], ALU.mult, ALU.add)
            nc.vector.tensor_tensor(r[:, hi], g_hi[:], own_hi[:], ALU.add)
            for c, cols in enumerate((lo, hi)):
                o = sb.tile([P, 256], F32, name="o%d%d" % (h, c))
                nc.vector.scalar_tensor_tensor(o[:], half_sc[:, cols], -0.4, r[:, cols], ALU.mult, ALU.max)
                nc.sync.dma_start(out[h * HALF : (h + 1) * HALF, cols], o[:])

        sc0 = hidden(0)
        for t in range(PACK):
            gather_sub(t, 1, t >= 1)
        sc1 = hidden(1)
        finish(0, sc0)
        finish(1, sc1)
